import numpy as np
import ml_dtypes


def mxq(x, axis, fmt="e4m3"):
    dtype, down = {"e4m3": (ml_dtypes.float8_e4m3fn, 7), "e5m2": (ml_dtypes.float8_e5m2, 14)}[fmt]
    v = np.moveaxis(np.asarray(x, np.float32).astype(ml_dtypes.bfloat16).astype(np.float64), axis, -1)
    blocks = v.reshape(v.shape[:-1] + (-1, 32))
    amax = np.abs(blocks).max(-1, keepdims=True)
    byte = np.maximum(np.where(amax > 0, np.frexp(amax)[1] - 1 + 127, 0) - down, 1)
    scale = np.exp2(byte - 127.0)
    codes = (blocks / scale).astype(np.float32).astype(dtype).astype(np.float64)
    return np.moveaxis((codes * scale).reshape(v.shape), -1, axis)


WIDE = False


def mx_kscale(k):
    if not WIDE:
        return np.ones(k)
    levels = np.array([10, -10, 5, -5, 0])
    if k % 512:
        return np.exp2(np.random.permutation(np.resize(levels, k // 32))).repeat(32)
    a = np.empty((k // 512, 16))
    for p in range(k // 512):
        a[p, :8] = np.random.permutation(np.resize(levels, 8))
        for g in range(8):
            far = levels[np.abs(levels - a[p, g]) >= 10]
            a[p, g + 8] = far[np.random.randint(len(far))]
    return np.exp2(a.ravel()).repeat(32)


def f64(x):
    return np.asarray(x).astype(np.float64)


def striped(idx):
    return np.tile(idx.reshape(-1, 16).T, (8, 1)).astype(np.uint16)


def unstriped(offs):
    return offs[:16].T.reshape(-1).astype(np.int64)


def pack_weight(w):
    k, n = w.shape
    w = f64(np.asarray(w, np.float32).astype(ml_dtypes.bfloat16)).reshape(k // 32, 32, n)
    amax = np.abs(w).max(1)
    byte = np.clip(np.where(amax > 0, np.frexp(amax)[1] - 1 + 127 - 7, 1), 1, 254)
    scaled = (w * np.exp2(127.0 - byte)[:, None, :]).reshape(k, n).astype(np.float32)
    words = np.ascontiguousarray(scaled.reshape(k // 512, 128, 4, n).transpose(0, 1, 3, 2)).astype(ml_dtypes.float8_e4m3fn).view(np.uint8)
    return words, np.ascontiguousarray(byte.astype(np.uint8).reshape(k // 512, 16, n))


def unpack_weight(words, scales):
    g, p, n, _ = words.shape
    vals = np.ascontiguousarray(words).view(ml_dtypes.float8_e4m3fn).astype(np.float64) * np.repeat(np.exp2(scales.astype(np.float64) - 127.0), 8, axis=1)[..., None]
    return vals.transpose(0, 1, 3, 2).reshape(g * 512, n)


E2M1 = np.array([0.0, 0.5, 1.0, 1.5, 2.0, 3.0, 4.0, 6.0, -0.0, -0.5, -1.0, -1.5, -2.0, -3.0, -4.0, -6.0])


def pack_fp4(w):
    k, n = w.shape
    w = f64(np.asarray(w, np.float32).astype(ml_dtypes.bfloat16)).reshape(k // 32, 32, n)
    amax = np.abs(w).max(1)
    mant, ex = np.frexp(amax / 6.0)
    byte = np.clip(np.where(amax > 0, np.where(mant > 0.5, ex, ex - 1) + 127, 1), 1, 254)
    scaled = (w * np.exp2(127.0 - byte)[:, None, :]).reshape(k, n).astype(np.float32)
    c = np.ascontiguousarray(scaled.reshape(k // 512, 128, 4, n).transpose(0, 1, 3, 2)).astype(ml_dtypes.float4_e2m1fn).view(np.uint8) & 0xF
    words = (c[..., 0::2] | (c[..., 1::2] << 4)).reshape(k // 512, 128, 2 * n)
    return np.ascontiguousarray(words), np.ascontiguousarray(byte.astype(np.uint8).reshape(k // 512, 16, n))


def unpack_fp4(words, scales):
    g, _, n = scales.shape
    words = np.ascontiguousarray(words).reshape(g, 128, n, 2)
    nib = np.empty((g, 128, n, 4), np.uint8)
    nib[..., 0::2] = words & 0xF
    nib[..., 1::2] = words >> 4
    vals = E2M1[nib] * np.repeat(np.exp2(scales.astype(np.float64) - 127.0), 8, axis=1)[..., None]
    return vals.transpose(0, 1, 3, 2).reshape(g * 512, n)


K, T, S, H, N = 512, 2048, 1024, 512, 128
P = 2 ** 7


def setup_inputs():
    n = np.random.standard_normal
    s = mx_kscale(K)[:, None]
    u = mx_kscale(H)
    packed_xT = pack_weight(n((K, T)) * s)
    packed_w2 = pack_fp4(n((H, N)) / np.sqrt(H) / u[:, None])
    return {
        "x_words": packed_xT[0],
        "x_scales": packed_xT[1],
        "w1": (n((K, H)) / np.sqrt(K) / s * u).astype(np.float32),
        "w2_words": packed_w2[0],
        "w2_scales": packed_w2[1],
        "lam": np.tile(np.random.uniform(0.1, 0.9, S), (P, 1)).astype(np.float32),
        "mu": np.tile(np.random.uniform(0.1, 0.9, S), (P, 1)).astype(np.float32),
        "offs": striped(np.random.permutation(T)[:S]),
        "pos1": striped(np.random.permutation(S)),
    }


def reference(x_words, x_scales, w1, w2_words, w2_scales, lam, mu, offs, pos1):
    xq = unpack_weight(x_words, x_scales)[:, unstriped(offs)]
    h = mxq(f64(w1), 0, "e4m3").T @ xq
    z = h * f64(lam)[:1] + h[:, unstriped(pos1)] * f64(mu)[:1]
    return unpack_fp4(w2_words, w2_scales).T @ mxq(z, 0, "e4m3")

@@ -1,0 +1,262 @@
+from contextlib import ExitStack
+
+import concourse.mybir as mybir
+from concourse.masks import make_identity
+
+K, T, S, H, N = 512, 2048, 1024, 512, 128
+FLOPS = 2 * K * H * S + 2 * H * N * S
+
+F32 = mybir.dt.float32
+BF16 = mybir.dt.bfloat16
+I32 = mybir.dt.int32
+U32 = mybir.dt.uint32
+U16 = mybir.dt.uint16
+U8 = mybir.dt.uint8
+FP8X4 = mybir.dt.float8_e4m3fn_x4
+FP4X4 = mybir.dt.float4_e2m1fn_x4
+COPY = mybir.ActivationFunctionType.Copy
+MULT = mybir.AluOpType.mult
+ADD = mybir.AluOpType.add
+
+P = 128
+PER_COLUMN = 16
+BLOCKS = S // P
+TILE_ORDER = (0, 2, 1, 3)
+CHUNKS = ((0,4), (4,8))
+GROUPS = ((0, 2), (2, 4), (4, 6), (6, 7), (7, 8))
+
+
+def tile_picked_mixup_none_p_kernel(
+    tc, x_words, x_scales, w1, w2_words, w2_scales, lam, mu, offs, pos1, out
+):
+    nc = tc.nc
+    with ExitStack() as ctx:
+        keep = ctx.enter_context(tc.tile_pool(name="keep", bufs=1))
+        psum = ctx.enter_context(tc.psum_pool(name="psum", bufs=1))
+
+        def bank(index, shape, name):
+            return psum.tile(shape, F32, name=name, tag="bank%d" % index)
+
+        def entries(lst, first, last):
+            return lst[:, first // PER_COLUMN : last // PER_COLUMN]
+
+        offs_sb = keep.tile([P, S // PER_COLUMN], U16, name="offs_sb")
+        pos_sb = keep.tile([P, S // PER_COLUMN], U16, name="pos_sb")
+        x_scale_rows = keep.tile([P, T], U8, name="x_scale_rows", align_bytes=64)
+        x_word_rows = keep.tile([P, T], U32, name="x_word_rows", align_bytes=64)
+        w1_raw = [keep.tile([P, 4, H // 2], F32, name="w1_raw%d" % a, tag="rows%d" % a, align_bytes=64) for a in range(2)]
+        w2_codes = keep.tile([P, 2 * N], U8, name="w2_codes", align_bytes=64)
+        w2_planes = keep.tile([P, N], U8, name="w2_planes", align_bytes=64)
+        shares = keep.tile([P, P], F32, name="shares")
+        ident = keep.tile([P, P], F32, name="ident")
+
+        nc.vector.memset(x_scale_rows[:].bitcast(I32), 0)
+        nc.gpsimd.memset(w2_planes[:].bitcast(I32), 0)
+        nc.gpsimd.memset(shares[:], 0.0)
+        make_identity(nc, ident[:])
+
+        w1_view = w1.rearrange("(p j) c -> p j c", j=4)
+        nc.sync.dma_start(offs_sb[:], offs)
+        nc.sync.dma_start(pos_sb[:], pos1)
+        for q in range(4):
+            nc.sync.dma_start(
+                x_scale_rows[32 * q : 32 * q + 4, :].bitcast(I32),
+                x_scales[0, 4 * q : 4 * q + 4, :].bitcast(I32),
+            )
+        nc.sync.dma_start(w1_raw[0][:], w1_view[:, :, 0 : H // 2])
+        nc.sync.dma_start(
+            x_word_rows[:].bitcast(I32),
+            x_words[0].rearrange("p n t -> p (n t)").bitcast(I32),
+        )
+        nc.sync.dma_start(w1_raw[1][:], w1_view[:, :, H // 2 : H])
+        nc.sync.dma_start(shares[0:BLOCKS, :], lam[0].rearrange("(b c) -> b c", c=P))
+        nc.sync.dma_start(shares[BLOCKS : 2 * BLOCKS, :], mu[0].rearrange("(b c) -> b c", c=P))
+        nc.sync.dma_start(w2_codes[:], w2_words[0])
+        for q in range(4):
+            nc.sync.dma_start(
+                w2_planes[32 * q : 32 * q + 4, :].bitcast(I32),
+                w2_scales[0, 4 * q : 4 * q + 4, :].bitcast(I32),
+            )
+
+        w1_bf = [keep.tile([P, 2, 64, 2, 4], BF16, name="w1_bf%d" % a, tag="rows%d" % (2 + a), align_bytes=64) for a in range(2)]
+        w1_codes = [keep.tile([P, 2 * P], U32, name="w1_codes%d" % a, align_bytes=64) for a in range(2)]
+        w1_planes = [keep.tile([P, 2 * P], U8, name="w1_planes%d" % a, align_bytes=64) for a in range(2)]
+
+        def round_w1(a):
+            src = w1_raw[a][:].rearrange("p j (q u e) -> p u q e j", u=2, e=2)
+            for u in range(2):
+                nc.scalar.activation(w1_bf[a][:, u], src[:, u], COPY)
+
+        def quantise_w1(a):
+            nc.vector.quantize_mx(
+                out=w1_codes[a][:].bitcast(FP8X4),
+                scales=w1_planes[a][:],
+                in_=w1_bf[a][:].rearrange("p u q e j -> p (u q e j)"),
+            )
+
+        x_planes = keep.tile([P, S], U8, name="x_planes", align_bytes=64)
+        x_codes = {}
+
+        def gather_words(first, last):
+            half, base = divmod(first, S // 2)
+            if half not in x_codes:
+                x_codes[half] = keep.tile(
+                    [P, S // 2], U32, name="x_codes%d" % half, tag=("rows2", "x_codes1")[half], align_bytes=64
+                )
+            nc.vector.tensor_copy(
+                x_codes[half][:, base : base + last - first],
+                x_word_rows[:].indirect(entries(offs_sb, first, last)),
+            )
+
+        h = {}
+
+        def first_product(t, first, last, bank_index, evacuate):
+            u, a = divmod(t, 2)
+            half, base = divmod(first, S // 2)
+            acc = bank(bank_index, [P, last - first], "h_acc")
+            nc.tensor.matmul_mx(
+                out=acc[:],
+                lhsT=w1_codes[a][:, u * P : (u + 1) * P].bitcast(FP8X4),
+                lhsT_scale=w1_planes[a][:, u * P : (u + 1) * P],
+                rhs=x_codes[half][:, base : base + last - first].bitcast(FP8X4),
+                rhs_scale=x_planes[:, first:last],
+                start=True,
+                stop=True,
+            )
+            if t not in h:
+                h[t] = keep.tile([P, S], F32, name="h%d" % t, tag="rows%d" % (1, 0, 3, 4)[t], align_bytes=64)
+            evacuate(h[t][:, first:last], acc[:])
+
+        nc.vector.tensor_copy(x_planes[:], x_scale_rows[:].indirect(offs_sb[:]))
+        round_w1(0)
+        quantise_w1(0)
+        gather_words(0, 512)
+        round_w1(1)
+        gather_words(512, 768)
+        gather_words(768, 1024)
+        quantise_w1(1)
+        first_product(0, 0, 512, 5, nc.scalar.copy)
+        first_product(0, 512, 768, 7, nc.scalar.copy)
+        first_product(0, 768, 1024, 0, nc.vector.tensor_copy)
+        first_product(2, 0, 512, 6, nc.scalar.copy)
+        first_product(2, 512, 1024, 5, nc.scalar.copy)
+        first_product(1, 0, 512, 7, nc.scalar.copy)
+        first_product(1, 512, 1024, 0, nc.scalar.copy)
+        first_product(3, 0, 512, 6, nc.scalar.copy)
+        first_product(3, 512, 1024, 5, nc.scalar.copy)
+
+        shares_turned = bank(4, [P, P], "shares_turned")
+        nc.tensor.transpose(shares_turned[:], shares[:], ident[:])
+        share_cols = keep.tile([P, 2 * BLOCKS], F32, name="share_cols")
+        nc.scalar.copy(share_cols[:], shares_turned[:, 0 : 2 * BLOCKS])
+
+        def block_bank(b):
+            return (1, 2, 3, 4, 7, 0, 6, 5)[b]
+
+        own = {}
+
+        def scale_own(b):
+            turned = bank(block_bank(b), [P, 4, P], "own_turned")
+            for t in TILE_ORDER:
+                nc.tensor.transpose(turned[:, t, :], h[t][:, b * P : (b + 1) * P], ident[:])
+            own[b] = keep.tile([P, H], F32, name="own%d" % b)
+            nc.scalar.activation(
+                own[b][:], turned[:].rearrange("p t c -> p (t c)"), COPY, scale=share_cols[:, b : b + 1]
+            )
+
+        partners = {}
+
+        def gather_partners(t, b0, b1, tag):
+            g = keep.tile([P, (b1 - b0) * P], F32, name="partner%d_%d" % (t, b0), tag=tag)
+            nc.vector.tensor_copy(g[:], h[t][:].indirect(entries(pos_sb, b0 * P, b1 * P)))
+            for b in range(b0, b1):
+                partners[(t, b)] = g[:, (b - b0) * P : (b - b0 + 1) * P]
+
+        partner_turned = {}
+
+        def turn_partner(t, b):
+            if b not in partner_turned:
+                partner_turned[b] = bank(block_bank(b), [P, 4, P], "partner_turned")
+            nc.tensor.transpose(partner_turned[b][:, t, :], partners[(t, b)], ident[:])
+
+        mixed = {}
+
+        def mix(b):
+            turn_partner(3, b)
+            mixed[b] = keep.tile([P, H], BF16, name="mixed%d" % b)
+            nc.vector.scalar_tensor_tensor(
+                mixed[b][:],
+                partner_turned[b][:].rearrange("p t c -> p (t c)"),
+                share_cols[:, BLOCKS + b : BLOCKS + b + 1],
+                own[b][:],
+                MULT,
+                ADD,
+            )
+
+        z_bf = {}
+
+        def turn_back(gi):
+            b0, b1 = GROUPS[gi]
+            n = b1 - b0
+            turned = bank(block_bank(b0), [P, n, 2, P], "z_turned")
+            for b in range(b0, b1):
+                words = mixed[b][:].bitcast(F32)
+                for u in range(2):
+                    nc.tensor.transpose(turned[:, b - b0, u, :], words[:, u * P : (u + 1) * P], ident[:])
+            z_bf[gi] = keep.tile([P, n * H], BF16, name="z_bf%d" % gi, align_bytes=64)
+            nc.scalar.copy(
+                z_bf[gi][:].bitcast(F32).rearrange("p (b j u) -> p b j u", b=n, u=2),
+                turned[:].rearrange("p b u j -> p b j u"),
+            )
+
+        def second_product(gi):
+            b0, b1 = GROUPS[gi]
+            width = (b1 - b0) * P
+            z_codes = keep.tile([P, width], U32, name="z_codes%d" % gi, align_bytes=64)
+            z_planes = keep.tile([P, width], U8, name="z_planes%d" % gi, align_bytes=64)
+            nc.vector.quantize_mx(out=z_codes[:].bitcast(FP8X4), scales=z_planes[:], in_=z_bf[gi][:])
+            acc = bank(block_bank(b1 - 1), [P, width], "out_acc")
+            nc.tensor.matmul_mx(
+                out=acc[:],
+                lhsT=w2_codes[:].bitcast(FP4X4),
+                lhsT_scale=w2_planes[:],
+                rhs=z_codes[:].bitcast(FP8X4),
+                rhs_scale=z_planes[:],
+                start=True,
+                stop=True,
+            )
+            result = keep.tile([P, width], F32, name="result%d" % gi)
+            nc.scalar.copy(result[:], acc[:])
+            nc.sync.dma_start(out[:, b0 * P : b1 * P], result[:])
+
+        for b in range(BLOCKS):
+            scale_own(b)
+        for b0, b1 in CHUNKS:
+            gather_partners(0, b0, b1, "first%d" % b0)
+        for t in (2, 1):
+            for b0 in (0, 4):
+                gather_partners(t, b0, b0 + 4, "mid%d_%d" % (t, b0))
+        for b in range(BLOCKS):
+            for t in (0, 2, 1):
+                turn_partner(t, b)
+        gather_partners(3, 0, 4, "last0")
+        gather_partners(3, 4, 6, "last4")
+        gather_partners(3, 6, 8, "last6")
+        mix(0)
+        mix(1)
+        turn_back(0)
+        mix(2)
+        mix(3)
+        turn_back(1)
+        second_product(0)
+        mix(4)
+        mix(5)
+        turn_back(2)
+        second_product(1)
+        mix(6)
+        turn_back(3)
+        mix(7)
+        turn_back(4)
+        second_product(2)
+        second_product(3)
+        second_product(4)

@@ -23,6 +23,8 @@ PER_COLUMN = 16
 BLOCKS = S // P
 TILE_ORDER = (0, 2, 1, 3)
 CHUNKS = ((0,4), (4,8))
+H_TAGS = ("h0", "rows0", "rows1", "h3")
+POOL_BLOCKS = ()
 GROUPS = ((0, 2), (2, 4), (4, 6), (6, 7), (7, 8))
 
 
@@ -59,15 +61,15 @@ def tile_picked_mixup_none_p_kernel(
         nc.sync.dma_start(offs_sb[:], offs)
         nc.sync.dma_start(pos_sb[:], pos1)
         for q in range(4):
-            nc.sync.dma_start(
+            (nc.sync, nc.scalar)[q % 2].dma_start(
                 x_scale_rows[32 * q : 32 * q + 4, :].bitcast(I32),
                 x_scales[0, 4 * q : 4 * q + 4, :].bitcast(I32),
             )
-        nc.sync.dma_start(w1_raw[0][:], w1_view[:, :, 0 : H // 2])
         nc.sync.dma_start(
             x_word_rows[:].bitcast(I32),
             x_words[0].rearrange("p n t -> p (n t)").bitcast(I32),
         )
+        nc.sync.dma_start(w1_raw[0][:], w1_view[:, :, 0 : H // 2])
         nc.sync.dma_start(w1_raw[1][:], w1_view[:, :, H // 2 : H])
         nc.sync.dma_start(shares[0:BLOCKS, :], lam[0].rearrange("(b c) -> b c", c=P))
         nc.sync.dma_start(shares[BLOCKS : 2 * BLOCKS, :], mu[0].rearrange("(b c) -> b c", c=P))
@@ -78,72 +80,69 @@ def tile_picked_mixup_none_p_kernel(
                 w2_scales[0, 4 * q : 4 * q + 4, :].bitcast(I32),
             )
 
-        w1_bf = [keep.tile([P, 2, 64, 2, 4], BF16, name="w1_bf%d" % a, tag="rows%d" % (2 + a), align_bytes=64) for a in range(2)]
-        w1_codes = [keep.tile([P, 2 * P], U32, name="w1_codes%d" % a, align_bytes=64) for a in range(2)]
-        w1_planes = [keep.tile([P, 2 * P], U8, name="w1_planes%d" % a, align_bytes=64) for a in range(2)]
+        w1_bf, w1_codes, w1_planes = {}, {}, {}
 
-        def round_w1(a):
+        def round_w1(t):
+            u, a = divmod(t, 2)
             src = w1_raw[a][:].rearrange("p j (q u e) -> p u q e j", u=2, e=2)
-            for u in range(2):
-                nc.scalar.activation(w1_bf[a][:, u], src[:, u], COPY)
+            w1_bf[t] = keep.tile([P, 64, 2, 4], BF16, name="w1_bf%d" % t, tag="w1_bf%d" % t, align_bytes=64)
+            nc.scalar.activation(w1_bf[t][:], src[:, u], COPY)
 
-        def quantise_w1(a):
+        def quantise_w1(t):
+            w1_codes[t] = keep.tile([P, P], U32, name="w1_codes%d" % t, align_bytes=64)
+            w1_planes[t] = keep.tile([P, P], U8, name="w1_planes%d" % t, align_bytes=64)
             nc.vector.quantize_mx(
-                out=w1_codes[a][:].bitcast(FP8X4),
-                scales=w1_planes[a][:],
-                in_=w1_bf[a][:].rearrange("p u q e j -> p (u q e j)"),
+                out=w1_codes[t][:].bitcast(FP8X4),
+                scales=w1_planes[t][:],
+                in_=w1_bf[t][:].rearrange("p q e j -> p (q e j)"),
             )
 
         x_planes = keep.tile([P, S], U8, name="x_planes", align_bytes=64)
         x_codes = {}
 
-        def gather_words(first, last):
-            half, base = divmod(first, S // 2)
-            if half not in x_codes:
-                x_codes[half] = keep.tile(
-                    [P, S // 2], U32, name="x_codes%d" % half, tag=("rows2", "x_codes1")[half], align_bytes=64
-                )
-            nc.vector.tensor_copy(
-                x_codes[half][:, base : base + last - first],
-                x_word_rows[:].indirect(entries(offs_sb, first, last)),
-            )
+        def gather_words(first, last, tag):
+            x_codes[first] = keep.tile([P, last - first], U32, name="x_codes%d" % first, tag=tag, align_bytes=64)
+            nc.vector.tensor_copy(x_codes[first][:], x_word_rows[:].indirect(entries(offs_sb, first, last)))
 
         h = {}
 
-        def first_product(t, first, last, bank_index, evacuate):
-            u, a = divmod(t, 2)
-            half, base = divmod(first, S // 2)
-            acc = bank(bank_index, [P, last - first], "h_acc")
-            nc.tensor.matmul_mx(
-                out=acc[:],
-                lhsT=w1_codes[a][:, u * P : (u + 1) * P].bitcast(FP8X4),
-                lhsT_scale=w1_planes[a][:, u * P : (u + 1) * P],
-                rhs=x_codes[half][:, base : base + last - first].bitcast(FP8X4),
-                rhs_scale=x_planes[:, first:last],
-                start=True,
-                stop=True,
-            )
+        def first_product(t, cuts, bank_index, evacuate):
+            acc = bank(bank_index, [P, cuts[-1] - cuts[0]], "h_acc")
+            for first, last in zip(cuts[:-1], cuts[1:]):
+                nc.tensor.matmul_mx(
+                    out=acc[:, first - cuts[0] : last - cuts[0]],
+                    lhsT=w1_codes[t][:].bitcast(FP8X4),
+                    lhsT_scale=w1_planes[t][:],
+                    rhs=x_codes[first][:].bitcast(FP8X4),
+                    rhs_scale=x_planes[:, first:last],
+                    start=True,
+                    stop=True,
+                )
             if t not in h:
-                h[t] = keep.tile([P, S], F32, name="h%d" % t, tag="rows%d" % (1, 0, 3, 4)[t], align_bytes=64)
-            evacuate(h[t][:, first:last], acc[:])
+                h[t] = keep.tile([P, S], F32, name="h%d" % t, tag=H_TAGS[t], align_bytes=64)
+            evacuate(h[t][:, cuts[0] : cuts[-1]], acc[:])
 
         nc.vector.tensor_copy(x_planes[:], x_scale_rows[:].indirect(offs_sb[:]))
+        gather_words(0, 512, "x_codes0")
+        gather_words(512, 768, "x_codes1")
         round_w1(0)
         quantise_w1(0)
-        gather_words(0, 512)
+        gather_words(768, 1024, "w1_bf0")
+        round_w1(2)
+        quantise_w1(2)
         round_w1(1)
-        gather_words(512, 768)
-        gather_words(768, 1024)
+        first_product(0, (0, 512), 5, nc.scalar.copy)
+        first_product(0, (512, 768), 7, nc.vector.tensor_copy)
+        first_product(0, (768, 1024), 0, nc.vector.tensor_copy)
+        round_w1(3)
         quantise_w1(1)
-        first_product(0, 0, 512, 5, nc.scalar.copy)
-        first_product(0, 512, 768, 7, nc.scalar.copy)
-        first_product(0, 768, 1024, 0, nc.vector.tensor_copy)
-        first_product(2, 0, 512, 6, nc.scalar.copy)
-        first_product(2, 512, 1024, 5, nc.scalar.copy)
-        first_product(1, 0, 512, 7, nc.scalar.copy)
-        first_product(1, 512, 1024, 0, nc.scalar.copy)
-        first_product(3, 0, 512, 6, nc.scalar.copy)
-        first_product(3, 512, 1024, 5, nc.scalar.copy)
+        quantise_w1(3)
+        first_product(2, (0, 512), 6, nc.scalar.copy)
+        first_product(2, (512, 768, 1024), 5, nc.scalar.copy)
+        first_product(1, (0, 512), 7, nc.scalar.copy)
+        first_product(1, (512, 768, 1024), 0, nc.scalar.copy)
+        first_product(3, (0, 512), 6, nc.scalar.copy)
+        first_product(3, (512, 768, 1024), 5, nc.scalar.copy)
 
         shares_turned = bank(4, [P, P], "shares_turned")
         nc.tensor.transpose(shares_turned[:], shares[:], ident[:])
@@ -167,7 +166,7 @@ def tile_picked_mixup_none_p_kernel(
         partners = {}
 
         def gather_partners(t, b0, b1, tag):
-            g = keep.tile([P, (b1 - b0) * P], F32, name="partner%d_%d" % (t, b0), tag=tag)
+            g = keep.tile([P, (b1 - b0) * P], F32, name="partner%d_%d" % (t, b0), tag=tag, align_bytes=64)
             nc.vector.tensor_copy(g[:], h[t][:].indirect(entries(pos_sb, b0 * P, b1 * P)))
             for b in range(b0, b1):
                 partners[(t, b)] = g[:, (b - b0) * P : (b - b0 + 1) * P]
@@ -184,6 +183,16 @@ def tile_picked_mixup_none_p_kernel(
         def mix(b):
             turn_partner(3, b)
             mixed[b] = keep.tile([P, H], BF16, name="mixed%d" % b)
+            if b in POOL_BLOCKS:
+                other = keep.tile([P, H], F32, name="other%d" % b)
+                nc.scalar.activation(
+                    other[:],
+                    partner_turned[b][:].rearrange("p t c -> p (t c)"),
+                    COPY,
+                    scale=share_cols[:, BLOCKS + b : BLOCKS + b + 1],
+                )
+                nc.gpsimd.tensor_add(mixed[b][:], own[b][:], other[:])
+                return
             nc.vector.scalar_tensor_tensor(
                 mixed[b][:],
                 partner_turned[b][:].rearrange("p t c -> p (t c)"),
@@ -231,17 +240,17 @@ def tile_picked_mixup_none_p_kernel(
 
         for b in range(BLOCKS):
             scale_own(b)
-        for b0, b1 in CHUNKS:
-            gather_partners(0, b0, b1, "first%d" % b0)
+        gather_partners(0, 0, 4, "f0")
+        gather_partners(0, 4, 8, "w1_bf3")
         for t in (2, 1):
             for b0 in (0, 4):
                 gather_partners(t, b0, b0 + 4, "mid%d_%d" % (t, b0))
         for b in range(BLOCKS):
             for t in (0, 2, 1):
                 turn_partner(t, b)
-        gather_partners(3, 0, 4, "last0")
-        gather_partners(3, 4, 6, "last4")
-        gather_partners(3, 6, 8, "last6")
+        gather_partners(3, 0, 4, "x")
+        gather_partners(3, 4, 6, "y")
+        gather_partners(3, 6, 8, "z")
         mix(0)
         mix(1)
         turn_back(0)

@@ -21,10 +21,16 @@ ADD = mybir.AluOpType.add
 P = 128
 PER_COLUMN = 16
 BLOCKS = S // P
-TILE_ORDER = (0, 2, 1, 3)
+TILE_ORDER = (0, 1, 2, 3)
 CHUNKS = ((0,4), (4,8))
-H_TAGS = ("h0", "rows0", "rows1", "h3")
+H_TAGS = ("rows2", "rows3", "rows0", "rows1")
 POOL_BLOCKS = ()
+Z_BANKS = (0, 2, 4, 6, 7)
+OUT_BANKS = (1, 3, 5, 0, 2)
+DIRECT_BLOCKS = ()
+PRODUCTS = ((0, 2), (2, 4), (4, 6), (6, 7), (7, 8))
+SCALAR_STORE = ()
+VECTOR_OUT = (3,)
 GROUPS = ((0, 2), (2, 4), (4, 6), (6, 7), (7, 8))
 
 
@@ -46,7 +52,7 @@ def tile_picked_mixup_none_p_kernel(
         pos_sb = keep.tile([P, S // PER_COLUMN], U16, name="pos_sb")
         x_scale_rows = keep.tile([P, T], U8, name="x_scale_rows", align_bytes=64)
         x_word_rows = keep.tile([P, T], U32, name="x_word_rows", align_bytes=64)
-        w1_raw = [keep.tile([P, 4, H // 2], F32, name="w1_raw%d" % a, tag="rows%d" % a, align_bytes=64) for a in range(2)]
+        w1_raw = [keep.tile([P, 4, P], F32, name="w1_raw%d" % t, tag="rows%d" % t, align_bytes=64) for t in range(4)]
         w2_codes = keep.tile([P, 2 * N], U8, name="w2_codes", align_bytes=64)
         w2_planes = keep.tile([P, N], U8, name="w2_planes", align_bytes=64)
         shares = keep.tile([P, P], F32, name="shares")
@@ -69,8 +75,8 @@ def tile_picked_mixup_none_p_kernel(
             x_word_rows[:].bitcast(I32),
             x_words[0].rearrange("p n t -> p (n t)").bitcast(I32),
         )
-        nc.sync.dma_start(w1_raw[0][:], w1_view[:, :, 0 : H // 2])
-        nc.sync.dma_start(w1_raw[1][:], w1_view[:, :, H // 2 : H])
+        for t in range(4):
+            nc.sync.dma_start(w1_raw[t][:], w1_view[:, :, t * P : (t + 1) * P])
         nc.sync.dma_start(shares[0:BLOCKS, :], lam[0].rearrange("(b c) -> b c", c=P))
         nc.sync.dma_start(shares[BLOCKS : 2 * BLOCKS, :], mu[0].rearrange("(b c) -> b c", c=P))
         nc.sync.dma_start(w2_codes[:], w2_words[0])
@@ -80,29 +86,38 @@ def tile_picked_mixup_none_p_kernel(
                 w2_scales[0, 4 * q : 4 * q + 4, :].bitcast(I32),
             )
 
-        w1_bf, w1_codes, w1_planes = {}, {}, {}
+        w1_bf = {}
+        w1_codes = keep.tile([P, H], U32, name="w1_codes", tag="w1_codes", align_bytes=64)
+        w1_planes = keep.tile([P, H], U8, name="w1_planes", tag="w1_planes", align_bytes=64)
 
         def round_w1(t):
-            u, a = divmod(t, 2)
-            src = w1_raw[a][:].rearrange("p j (q u e) -> p u q e j", u=2, e=2)
-            w1_bf[t] = keep.tile([P, 64, 2, 4], BF16, name="w1_bf%d" % t, tag="w1_bf%d" % t, align_bytes=64)
-            nc.scalar.activation(w1_bf[t][:], src[:, u], COPY)
+            w1_bf[t] = keep.tile([P, 2, 32, 8], BF16, name="w1_bf%d" % t, tag="w1_bf%d" % t, align_bytes=64)
+            nc.scalar.activation(
+                w1_bf[t][:].rearrange("p u q (e j) -> p q u e j", e=2),
+                w1_raw[t][:].rearrange("p j (q u e) -> p q u e j", u=2, e=2),
+                COPY,
+            )
 
         def quantise_w1(t):
-            w1_codes[t] = keep.tile([P, P], U32, name="w1_codes%d" % t, align_bytes=64)
-            w1_planes[t] = keep.tile([P, P], U8, name="w1_planes%d" % t, align_bytes=64)
             nc.vector.quantize_mx(
-                out=w1_codes[t][:].bitcast(FP8X4),
-                scales=w1_planes[t][:],
-                in_=w1_bf[t][:].rearrange("p q e j -> p (q e j)"),
+                out=w1_codes[:, t * P : (t + 1) * P].bitcast(FP8X4),
+                scales=w1_planes[:, t * P : (t + 1) * P],
+                in_=w1_bf[t][:].rearrange("p u q c -> p (u q c)"),
             )
 
         x_planes = keep.tile([P, S], U8, name="x_planes", align_bytes=64)
         x_codes = {}
 
-        def gather_words(first, last, tag):
-            x_codes[first] = keep.tile([P, last - first], U32, name="x_codes%d" % first, tag=tag, align_bytes=64)
-            nc.vector.tensor_copy(x_codes[first][:], x_word_rows[:].indirect(entries(offs_sb, first, last)))
+        def picked_words(first, last):
+            half, base = divmod(first, S // 2)
+            if half not in x_codes:
+                x_codes[half] = keep.tile(
+                    [P, S // 2], U32, name="x_codes%d" % half, tag=("x_codes0", "w1_bf0")[half], align_bytes=64
+                )
+            return x_codes[half][:, base : base + last - first]
+
+        def gather_words(first, last):
+            nc.vector.tensor_copy(picked_words(first, last), x_word_rows[:].indirect(entries(offs_sb, first, last)))
 
         h = {}
 
@@ -111,9 +126,9 @@ def tile_picked_mixup_none_p_kernel(
             for first, last in zip(cuts[:-1], cuts[1:]):
                 nc.tensor.matmul_mx(
                     out=acc[:, first - cuts[0] : last - cuts[0]],
-                    lhsT=w1_codes[t][:].bitcast(FP8X4),
-                    lhsT_scale=w1_planes[t][:],
-                    rhs=x_codes[first][:].bitcast(FP8X4),
+                    lhsT=w1_codes[:, t * P : (t + 1) * P].bitcast(FP8X4),
+                    lhsT_scale=w1_planes[:, t * P : (t + 1) * P],
+                    rhs=picked_words(first, last).bitcast(FP8X4),
                     rhs_scale=x_planes[:, first:last],
                     start=True,
                     stop=True,
@@ -123,26 +138,26 @@ def tile_picked_mixup_none_p_kernel(
             evacuate(h[t][:, cuts[0] : cuts[-1]], acc[:])
 
         nc.vector.tensor_copy(x_planes[:], x_scale_rows[:].indirect(offs_sb[:]))
-        gather_words(0, 512, "x_codes0")
-        gather_words(512, 768, "x_codes1")
+        gather_words(0, 512)
         round_w1(0)
         quantise_w1(0)
-        gather_words(768, 1024, "w1_bf0")
+        gather_words(512, 768)
+        gather_words(768, 1024)
+        round_w1(1)
+        quantise_w1(1)
         round_w1(2)
         quantise_w1(2)
-        round_w1(1)
         first_product(0, (0, 512), 5, nc.scalar.copy)
-        first_product(0, (512, 768), 7, nc.vector.tensor_copy)
+        first_product(0, (512, 768), 7, nc.scalar.copy)
         first_product(0, (768, 1024), 0, nc.vector.tensor_copy)
         round_w1(3)
-        quantise_w1(1)
         quantise_w1(3)
-        first_product(2, (0, 512), 6, nc.scalar.copy)
-        first_product(2, (512, 768, 1024), 5, nc.scalar.copy)
-        first_product(1, (0, 512), 7, nc.scalar.copy)
-        first_product(1, (512, 768, 1024), 0, nc.scalar.copy)
+        first_product(1, (0, 512), 6, nc.scalar.copy)
+        first_product(1, (512, 1024), 5, nc.scalar.copy)
+        first_product(2, (0, 512), 7, nc.scalar.copy)
+        first_product(2, (512, 1024), 0, nc.scalar.copy)
         first_product(3, (0, 512), 6, nc.scalar.copy)
-        first_product(3, (512, 768, 1024), 5, nc.scalar.copy)
+        first_product(3, (512, 1024), 5, nc.scalar.copy)
 
         shares_turned = bank(4, [P, P], "shares_turned")
         nc.tensor.transpose(shares_turned[:], shares[:], ident[:])
@@ -155,12 +170,24 @@ def tile_picked_mixup_none_p_kernel(
         own = {}
 
         def scale_own(b):
-            turned = bank(block_bank(b), [P, 4, P], "own_turned")
-            for t in TILE_ORDER:
-                nc.tensor.transpose(turned[:, t, :], h[t][:, b * P : (b + 1) * P], ident[:])
+            turned = bank(block_bank(b), [P, 2, 4, 64], "own_turned")
+            if b in DIRECT_BLOCKS:
+                base = b * P - 768
+                nc.tensor.matmul_mx(
+                    out=turned[:].rearrange("p u t c -> p (u t c)"),
+                    lhsT=x_codes[768][:, base : base + P].bitcast(FP8X4),
+                    lhsT_scale=x_planes[:, b * P : (b + 1) * P],
+                    rhs=w1_codes[:].bitcast(FP8X4),
+                    rhs_scale=w1_planes[:],
+                    start=True,
+                    stop=True,
+                )
+            else:
+                for t in TILE_ORDER:
+                    nc.tensor.transpose(turned[:, :, t, :], h[t][:, b * P : (b + 1) * P], ident[:])
             own[b] = keep.tile([P, H], F32, name="own%d" % b)
             nc.scalar.activation(
-                own[b][:], turned[:].rearrange("p t c -> p (t c)"), COPY, scale=share_cols[:, b : b + 1]
+                own[b][:], turned[:].rearrange("p u t c -> p (u t c)"), COPY, scale=share_cols[:, b : b + 1]
             )
 
         partners = {}
@@ -175,19 +202,18 @@ def tile_picked_mixup_none_p_kernel(
 
         def turn_partner(t, b):
             if b not in partner_turned:
-                partner_turned[b] = bank(block_bank(b), [P, 4, P], "partner_turned")
-            nc.tensor.transpose(partner_turned[b][:, t, :], partners[(t, b)], ident[:])
+                partner_turned[b] = bank(block_bank(b), [P, 2, 4, 64], "partner_turned")
+            nc.tensor.transpose(partner_turned[b][:, :, t, :], partners[(t, b)], ident[:])
 
         mixed = {}
 
         def mix(b):
-            turn_partner(3, b)
             mixed[b] = keep.tile([P, H], BF16, name="mixed%d" % b)
             if b in POOL_BLOCKS:
                 other = keep.tile([P, H], F32, name="other%d" % b)
                 nc.scalar.activation(
                     other[:],
-                    partner_turned[b][:].rearrange("p t c -> p (t c)"),
+                    partner_turned[b][:].rearrange("p u t c -> p (u t c)"),
                     COPY,
                     scale=share_cols[:, BLOCKS + b : BLOCKS + b + 1],
                 )
@@ -195,7 +221,7 @@ def tile_picked_mixup_none_p_kernel(
                 return
             nc.vector.scalar_tensor_tensor(
                 mixed[b][:],
-                partner_turned[b][:].rearrange("p t c -> p (t c)"),
+                partner_turned[b][:].rearrange("p u t c -> p (u t c)"),
                 share_cols[:, BLOCKS + b : BLOCKS + b + 1],
                 own[b][:],
                 MULT,
@@ -207,24 +233,27 @@ def tile_picked_mixup_none_p_kernel(
         def turn_back(gi):
             b0, b1 = GROUPS[gi]
             n = b1 - b0
-            turned = bank(block_bank(b0), [P, n, 2, P], "z_turned")
+            turned = bank(block_bank(Z_BANKS[gi]), [P, n, 2, P], "z_turned")
             for b in range(b0, b1):
                 words = mixed[b][:].bitcast(F32)
                 for u in range(2):
                     nc.tensor.transpose(turned[:, b - b0, u, :], words[:, u * P : (u + 1) * P], ident[:])
-            z_bf[gi] = keep.tile([P, n * H], BF16, name="z_bf%d" % gi, align_bytes=64)
+            pi = [i for i, (p0, p1) in enumerate(PRODUCTS) if p0 <= b0 < p1][0]
+            p0, p1 = PRODUCTS[pi]
+            if pi not in z_bf:
+                z_bf[pi] = keep.tile([P, (p1 - p0) * H], BF16, name="z_bf%d" % pi, align_bytes=64)
             nc.scalar.copy(
-                z_bf[gi][:].bitcast(F32).rearrange("p (b j u) -> p b j u", b=n, u=2),
+                z_bf[pi][:, (b0 - p0) * H : (b1 - p0) * H].bitcast(F32).rearrange("p (b j u) -> p b j u", b=n, u=2),
                 turned[:].rearrange("p b u j -> p b j u"),
             )
 
         def second_product(gi):
-            b0, b1 = GROUPS[gi]
+            b0, b1 = PRODUCTS[gi]
             width = (b1 - b0) * P
             z_codes = keep.tile([P, width], U32, name="z_codes%d" % gi, align_bytes=64)
             z_planes = keep.tile([P, width], U8, name="z_planes%d" % gi, align_bytes=64)
             nc.vector.quantize_mx(out=z_codes[:].bitcast(FP8X4), scales=z_planes[:], in_=z_bf[gi][:])
-            acc = bank(block_bank(b1 - 1), [P, width], "out_acc")
+            acc = bank(block_bank(OUT_BANKS[gi]), [P, width], "out_acc")
             nc.tensor.matmul_mx(
                 out=acc[:],
                 lhsT=w2_codes[:].bitcast(FP4X4),
@@ -235,37 +264,73 @@ def tile_picked_mixup_none_p_kernel(
                 stop=True,
             )
             result = keep.tile([P, width], F32, name="result%d" % gi)
-            nc.scalar.copy(result[:], acc[:])
-            nc.sync.dma_start(out[:, b0 * P : b1 * P], result[:])
+            (nc.vector.tensor_copy if gi in VECTOR_OUT else nc.scalar.copy)(result[:], acc[:])
+            (nc.scalar if gi in SCALAR_STORE else nc.sync).dma_start(out[:, b0 * P : b1 * P], result[:])
 
-        for b in range(BLOCKS):
-            scale_own(b)
-        gather_partners(0, 0, 4, "f0")
+        scale_own(0)
+        scale_own(1)
+        scale_own(2)
+        scale_own(3)
+        scale_own(4)
+        scale_own(5)
+        scale_own(6)
+        scale_own(7)
+        gather_partners(0, 0, 4, "a")
         gather_partners(0, 4, 8, "w1_bf3")
-        for t in (2, 1):
-            for b0 in (0, 4):
-                gather_partners(t, b0, b0 + 4, "mid%d_%d" % (t, b0))
-        for b in range(BLOCKS):
-            for t in (0, 2, 1):
-                turn_partner(t, b)
-        gather_partners(3, 0, 4, "x")
-        gather_partners(3, 4, 6, "y")
-        gather_partners(3, 6, 8, "z")
+        gather_partners(1, 0, 4, "b")
+        gather_partners(1, 4, 8, "c")
+        gather_partners(2, 0, 4, "d")
+        gather_partners(2, 4, 8, "e")
+        for t in (0, 1, 2,):
+            turn_partner(t, 0)
+        for t in (0, 1, 2,):
+            turn_partner(t, 1)
+        for t in (0, 1, 2,):
+            turn_partner(t, 2)
+        for t in (0, 1, 2,):
+            turn_partner(t, 3)
+        for t in (0, 1, 2,):
+            turn_partner(t, 4)
+        for t in (0, 1, 2,):
+            turn_partner(t, 5)
+        for t in (0, 1, 2,):
+            turn_partner(t, 6)
+        for t in (0, 1, 2,):
+            turn_partner(t, 7)
+        gather_partners(3, 0, 4, "d")
+        gather_partners(3, 4, 6, "g")
+        gather_partners(3, 6, 8, "h")
+        for t in (3,):
+            turn_partner(t, 0)
+        for t in (3,):
+            turn_partner(t, 1)
+        for t in (3,):
+            turn_partner(t, 2)
+        for t in (3,):
+            turn_partner(t, 3)
+        for t in (3,):
+            turn_partner(t, 4)
+        for t in (3,):
+            turn_partner(t, 5)
+        for t in (3,):
+            turn_partner(t, 6)
+        for t in (3,):
+            turn_partner(t, 7)
         mix(0)
         mix(1)
         turn_back(0)
         mix(2)
         mix(3)
         turn_back(1)
-        second_product(0)
         mix(4)
         mix(5)
         turn_back(2)
-        second_product(1)
         mix(6)
         turn_back(3)
         mix(7)
         turn_back(4)
+        second_product(0)
+        second_product(1)
         second_product(2)
         second_product(3)
         second_product(4)

@@ -24,14 +24,14 @@ BLOCKS = S // P
 TILE_ORDER = (0, 1, 2, 3)
 CHUNKS = ((0,4), (4,8))
 H_TAGS = ("rows2", "rows3", "rows0", "rows1")
-POOL_BLOCKS = ()
-Z_BANKS = (0, 2, 4, 6, 7)
-OUT_BANKS = (1, 3, 5, 0, 2)
+POOL_BLOCKS = (4, 5)
+Z_BANKS = (4, 6, 0, 2, 3)
+OUT_BANKS = (5, 7, 1, 4, 6)
 DIRECT_BLOCKS = ()
-PRODUCTS = ((0, 2), (2, 4), (4, 6), (6, 7), (7, 8))
+PRODUCTS = ((4, 6), (6, 8), (0, 2), (2, 3), (3, 4))
 SCALAR_STORE = ()
 VECTOR_OUT = (3,)
-GROUPS = ((0, 2), (2, 4), (4, 6), (6, 7), (7, 8))
+GROUPS = ((4, 6), (6, 8), (0, 2), (2, 3), (3, 4))
 
 
 def tile_picked_mixup_none_p_kernel(
@@ -280,7 +280,8 @@ def tile_picked_mixup_none_p_kernel(
         gather_partners(1, 0, 4, "b")
         gather_partners(1, 4, 8, "c")
         gather_partners(2, 0, 4, "d")
-        gather_partners(2, 4, 8, "e")
+        gather_partners(2, 4, 6, "e")
+        gather_partners(2, 6, 8, "e2")
         for t in (0, 1, 2,):
             turn_partner(t, 0)
         for t in (0, 1, 2,):
@@ -297,18 +298,9 @@ def tile_picked_mixup_none_p_kernel(
             turn_partner(t, 6)
         for t in (0, 1, 2,):
             turn_partner(t, 7)
-        gather_partners(3, 0, 4, "d")
         gather_partners(3, 4, 6, "g")
         gather_partners(3, 6, 8, "h")
         for t in (3,):
-            turn_partner(t, 0)
-        for t in (3,):
-            turn_partner(t, 1)
-        for t in (3,):
-            turn_partner(t, 2)
-        for t in (3,):
-            turn_partner(t, 3)
-        for t in (3,):
             turn_partner(t, 4)
         for t in (3,):
             turn_partner(t, 5)
@@ -316,18 +308,27 @@ def tile_picked_mixup_none_p_kernel(
             turn_partner(t, 6)
         for t in (3,):
             turn_partner(t, 7)
-        mix(0)
-        mix(1)
-        turn_back(0)
-        mix(2)
-        mix(3)
-        turn_back(1)
+        gather_partners(3, 0, 4, "e")
+        for t in (3,):
+            turn_partner(t, 0)
+        for t in (3,):
+            turn_partner(t, 1)
+        for t in (3,):
+            turn_partner(t, 2)
+        for t in (3,):
+            turn_partner(t, 3)
         mix(4)
         mix(5)
-        turn_back(2)
+        turn_back(0)
         mix(6)
-        turn_back(3)
         mix(7)
+        turn_back(1)
+        mix(0)
+        mix(1)
+        turn_back(2)
+        mix(2)
+        turn_back(3)
+        mix(3)
         turn_back(4)
         second_product(0)
         second_product(1)

from contextlib import ExitStack

import concourse.mybir as mybir
from concourse.masks import make_identity

K, T, S, H, N = 512, 2048, 1024, 512, 128
FLOPS = 2 * K * H * S + 2 * H * N * S

F32 = mybir.dt.float32
BF16 = mybir.dt.bfloat16
I32 = mybir.dt.int32
U32 = mybir.dt.uint32
U16 = mybir.dt.uint16
U8 = mybir.dt.uint8
FP8X4 = mybir.dt.float8_e4m3fn_x4
FP4X4 = mybir.dt.float4_e2m1fn_x4
COPY = mybir.ActivationFunctionType.Copy
MULT = mybir.AluOpType.mult
ADD = mybir.AluOpType.add

P = 128
PER_COLUMN = 16
BLOCKS = S // P
TILE_ORDER = (0, 1, 2, 3)
CHUNKS = ((0,4), (4,8))
H_TAGS = ("rows2", "rows3", "rows0", "rows1")
POOL_BLOCKS = (4, 5)
Z_BANKS = (4, 6, 0, 2, 3)
OUT_BANKS = (5, 7, 1, 4, 6)
DIRECT_BLOCKS = ()
PRODUCTS = ((4, 6), (6, 8), (0, 2), (2, 3), (3, 4))
SCALAR_STORE = ()
VECTOR_OUT = (3,)
GROUPS = ((4, 6), (6, 8), (0, 2), (2, 3), (3, 4))


def tile_picked_mixup_none_p_kernel(
    tc, x_words, x_scales, w1, w2_words, w2_scales, lam, mu, offs, pos1, out
):
    nc = tc.nc
    with ExitStack() as ctx:
        keep = ctx.enter_context(tc.tile_pool(name="keep", bufs=1))
        psum = ctx.enter_context(tc.psum_pool(name="psum", bufs=1))

        def bank(index, shape, name):
            return psum.tile(shape, F32, name=name, tag="bank%d" % index)

        def entries(lst, first, last):
            return lst[:, first // PER_COLUMN : last // PER_COLUMN]

        offs_sb = keep.tile([P, S // PER_COLUMN], U16, name="offs_sb")
        pos_sb = keep.tile([P, S // PER_COLUMN], U16, name="pos_sb")
        x_scale_rows = keep.tile([P, T], U8, name="x_scale_rows", align_bytes=64)
        x_word_rows = keep.tile([P, T], U32, name="x_word_rows", align_bytes=64)
        w1_raw = [keep.tile([P, 4, P], F32, name="w1_raw%d" % t, tag="rows%d" % t, align_bytes=64) for t in range(4)]
        w2_codes = keep.tile([P, 2 * N], U8, name="w2_codes", align_bytes=64)
        w2_planes = keep.tile([P, N], U8, name="w2_planes", align_bytes=64)
        shares = keep.tile([P, P], F32, name="shares")
        ident = keep.tile([P, P], F32, name="ident")

        nc.vector.memset(x_scale_rows[:].bitcast(I32), 0)
        nc.gpsimd.memset(w2_planes[:].bitcast(I32), 0)
        nc.gpsimd.memset(shares[:], 0.0)
        make_identity(nc, ident[:])

        w1_view = w1.rearrange("(p j) c -> p j c", j=4)
        nc.sync.dma_start(offs_sb[:], offs)
        nc.sync.dma_start(pos_sb[:], pos1)
        for q in range(4):
            (nc.sync, nc.scalar)[q % 2].dma_start(
                x_scale_rows[32 * q : 32 * q + 4, :].bitcast(I32),
                x_scales[0, 4 * q : 4 * q + 4, :].bitcast(I32),
            )
        nc.sync.dma_start(
            x_word_rows[:].bitcast(I32),
            x_words[0].rearrange("p n t -> p (n t)").bitcast(I32),
        )
        for t in range(4):
            nc.sync.dma_start(w1_raw[t][:], w1_view[:, :, t * P : (t + 1) * P])
        nc.sync.dma_start(shares[0:BLOCKS, :], lam[0].rearrange("(b c) -> b c", c=P))
        nc.sync.dma_start(shares[BLOCKS : 2 * BLOCKS, :], mu[0].rearrange("(b c) -> b c", c=P))
        nc.sync.dma_start(w2_codes[:], w2_words[0])
        for q in range(4):
            nc.sync.dma_start(
                w2_planes[32 * q : 32 * q + 4, :].bitcast(I32),
                w2_scales[0, 4 * q : 4 * q + 4, :].bitcast(I32),
            )

        w1_bf = {}
        w1_codes = keep.tile([P, H], U32, name="w1_codes", tag="w1_codes", align_bytes=64)
        w1_planes = keep.tile([P, H], U8, name="w1_planes", tag="w1_planes", align_bytes=64)

        def round_w1(t):
            w1_bf[t] = keep.tile([P, 2, 32, 8], BF16, name="w1_bf%d" % t, tag="w1_bf%d" % t, align_bytes=64)
            nc.scalar.activation(
                w1_bf[t][:].rearrange("p u q (e j) -> p q u e j", e=2),
                w1_raw[t][:].rearrange("p j (q u e) -> p q u e j", u=2, e=2),
                COPY,
            )

        def quantise_w1(t):
            nc.vector.quantize_mx(
                out=w1_codes[:, t * P : (t + 1) * P].bitcast(FP8X4),
                scales=w1_planes[:, t * P : (t + 1) * P],
                in_=w1_bf[t][:].rearrange("p u q c -> p (u q c)"),
            )

        x_planes = keep.tile([P, S], U8, name="x_planes", align_bytes=64)
        x_codes = {}

        def picked_words(first, last):
            half, base = divmod(first, S // 2)
            if half not in x_codes:
                x_codes[half] = keep.tile(
                    [P, S // 2], U32, name="x_codes%d" % half, tag=("x_codes0", "w1_bf0")[half], align_bytes=64
                )
            return x_codes[half][:, base : base + last - first]

        def gather_words(first, last):
            nc.vector.tensor_copy(picked_words(first, last), x_word_rows[:].indirect(entries(offs_sb, first, last)))

        h = {}

        def first_product(t, cuts, bank_index, evacuate):
            acc = bank(bank_index, [P, cuts[-1] - cuts[0]], "h_acc")
            for first, last in zip(cuts[:-1], cuts[1:]):
                nc.tensor.matmul_mx(
                    out=acc[:, first - cuts[0] : last - cuts[0]],
                    lhsT=w1_codes[:, t * P : (t + 1) * P].bitcast(FP8X4),
                    lhsT_scale=w1_planes[:, t * P : (t + 1) * P],
                    rhs=picked_words(first, last).bitcast(FP8X4),
                    rhs_scale=x_planes[:, first:last],
                    start=True,
                    stop=True,
                )
            if t not in h:
                h[t] = keep.tile([P, S], F32, name="h%d" % t, tag=H_TAGS[t], align_bytes=64)
            evacuate(h[t][:, cuts[0] : cuts[-1]], acc[:])

        nc.vector.tensor_copy(x_planes[:], x_scale_rows[:].indirect(offs_sb[:]))
        gather_words(0, 512)
        round_w1(0)
        quantise_w1(0)
        gather_words(512, 768)
        gather_words(768, 1024)
        round_w1(1)
        quantise_w1(1)
        round_w1(2)
        quantise_w1(2)
        first_product(0, (0, 512), 5, nc.scalar.copy)
        first_product(0, (512, 768), 7, nc.scalar.copy)
        first_product(0, (768, 1024), 0, nc.vector.tensor_copy)
        round_w1(3)
        quantise_w1(3)
        first_product(1, (0, 512), 6, nc.scalar.copy)
        first_product(1, (512, 1024), 5, nc.scalar.copy)
        first_product(2, (0, 512), 7, nc.scalar.copy)
        first_product(2, (512, 1024), 0, nc.scalar.copy)
        first_product(3, (0, 512), 6, nc.scalar.copy)
        first_product(3, (512, 1024), 5, nc.scalar.copy)

        shares_turned = bank(4, [P, P], "shares_turned")
        nc.tensor.transpose(shares_turned[:], shares[:], ident[:])
        share_cols = keep.tile([P, 2 * BLOCKS], F32, name="share_cols")
        nc.scalar.copy(share_cols[:], shares_turned[:, 0 : 2 * BLOCKS])

        def block_bank(b):
            return (1, 2, 3, 4, 7, 0, 6, 5)[b]

        own = {}

        def scale_own(b):
            turned = bank(block_bank(b), [P, 2, 4, 64], "own_turned")
            if b in DIRECT_BLOCKS:
                base = b * P - 768
                nc.tensor.matmul_mx(
                    out=turned[:].rearrange("p u t c -> p (u t c)"),
                    lhsT=x_codes[768][:, base : base + P].bitcast(FP8X4),
                    lhsT_scale=x_planes[:, b * P : (b + 1) * P],
                    rhs=w1_codes[:].bitcast(FP8X4),
                    rhs_scale=w1_planes[:],
                    start=True,
                    stop=True,
                )
            else:
                for t in TILE_ORDER:
                    nc.tensor.transpose(turned[:, :, t, :], h[t][:, b * P : (b + 1) * P], ident[:])
            own[b] = keep.tile([P, H], F32, name="own%d" % b)
            nc.scalar.activation(
                own[b][:], turned[:].rearrange("p u t c -> p (u t c)"), COPY, scale=share_cols[:, b : b + 1]
            )

        partners = {}

        def gather_partners(t, b0, b1, tag):
            g = keep.tile([P, (b1 - b0) * P], F32, name="partner%d_%d" % (t, b0), tag=tag, align_bytes=64)
            nc.vector.tensor_copy(g[:], h[t][:].indirect(entries(pos_sb, b0 * P, b1 * P)))
            for b in range(b0, b1):
                partners[(t, b)] = g[:, (b - b0) * P : (b - b0 + 1) * P]

        partner_turned = {}

        def turn_partner(t, b):
            if b not in partner_turned:
                partner_turned[b] = bank(block_bank(b), [P, 2, 4, 64], "partner_turned")
            nc.tensor.transpose(partner_turned[b][:, :, t, :], partners[(t, b)], ident[:])

        mixed = {}

        def mix(b):
            mixed[b] = keep.tile([P, H], BF16, name="mixed%d" % b)
            if b in POOL_BLOCKS:
                other = keep.tile([P, H], F32, name="other%d" % b)
                nc.scalar.activation(
                    other[:],
                    partner_turned[b][:].rearrange("p u t c -> p (u t c)"),
                    COPY,
                    scale=share_cols[:, BLOCKS + b : BLOCKS + b + 1],
                )
                nc.gpsimd.tensor_add(mixed[b][:], own[b][:], other[:])
                return
            nc.vector.scalar_tensor_tensor(
                mixed[b][:],
                partner_turned[b][:].rearrange("p u t c -> p (u t c)"),
                share_cols[:, BLOCKS + b : BLOCKS + b + 1],
                own[b][:],
                MULT,
                ADD,
            )

        z_bf = {}

        def turn_back(gi):
            b0, b1 = GROUPS[gi]
            n = b1 - b0
            turned = bank(block_bank(Z_BANKS[gi]), [P, n, 2, P], "z_turned")
            for b in range(b0, b1):
                words = mixed[b][:].bitcast(F32)
                for u in range(2):
                    nc.tensor.transpose(turned[:, b - b0, u, :], words[:, u * P : (u + 1) * P], ident[:])
            pi = [i for i, (p0, p1) in enumerate(PRODUCTS) if p0 <= b0 < p1][0]
            p0, p1 = PRODUCTS[pi]
            if pi not in z_bf:
                z_bf[pi] = keep.tile([P, (p1 - p0) * H], BF16, name="z_bf%d" % pi, align_bytes=64)
            nc.scalar.copy(
                z_bf[pi][:, (b0 - p0) * H : (b1 - p0) * H].bitcast(F32).rearrange("p (b j u) -> p b j u", b=n, u=2),
                turned[:].rearrange("p b u j -> p b j u"),
            )

        def second_product(gi):
            b0, b1 = PRODUCTS[gi]
            width = (b1 - b0) * P
            z_codes = keep.tile([P, width], U32, name="z_codes%d" % gi, align_bytes=64)
            z_planes = keep.tile([P, width], U8, name="z_planes%d" % gi, align_bytes=64)
            nc.vector.quantize_mx(out=z_codes[:].bitcast(FP8X4), scales=z_planes[:], in_=z_bf[gi][:])
            acc = bank(block_bank(OUT_BANKS[gi]), [P, width], "out_acc")
            nc.tensor.matmul_mx(
                out=acc[:],
                lhsT=w2_codes[:].bitcast(FP4X4),
                lhsT_scale=w2_planes[:],
                rhs=z_codes[:].bitcast(FP8X4),
                rhs_scale=z_planes[:],
                start=True,
                stop=True,
            )
            result = keep.tile([P, width], F32, name="result%d" % gi)
            (nc.vector.tensor_copy if gi in VECTOR_OUT else nc.scalar.copy)(result[:], acc[:])
            (nc.scalar if gi in SCALAR_STORE else nc.sync).dma_start(out[:, b0 * P : b1 * P], result[:])

        scale_own(0)
        scale_own(1)
        scale_own(2)
        scale_own(3)
        scale_own(4)
        scale_own(5)
        scale_own(6)
        scale_own(7)
        gather_partners(0, 0, 4, "a")
        gather_partners(0, 4, 8, "w1_bf3")
        gather_partners(1, 0, 4, "b")
        gather_partners(1, 4, 8, "c")
        gather_partners(2, 0, 4, "d")
        gather_partners(2, 4, 6, "e")
        gather_partners(2, 6, 8, "e2")
        for t in (0, 1, 2,):
            turn_partner(t, 0)
        for t in (0, 1, 2,):
            turn_partner(t, 1)
        for t in (0, 1, 2,):
            turn_partner(t, 2)
        for t in (0, 1, 2,):
            turn_partner(t, 3)
        for t in (0, 1, 2,):
            turn_partner(t, 4)
        for t in (0, 1, 2,):
            turn_partner(t, 5)
        for t in (0, 1, 2,):
            turn_partner(t, 6)
        for t in (0, 1, 2,):
            turn_partner(t, 7)
        gather_partners(3, 4, 6, "g")
        gather_partners(3, 6, 8, "h")
        for t in (3,):
            turn_partner(t, 4)
        for t in (3,):
            turn_partner(t, 5)
        for t in (3,):
            turn_partner(t, 6)
        for t in (3,):
            turn_partner(t, 7)
        gather_partners(3, 0, 4, "e")
        for t in (3,):
            turn_partner(t, 0)
        for t in (3,):
            turn_partner(t, 1)
        for t in (3,):
            turn_partner(t, 2)
        for t in (3,):
            turn_partner(t, 3)
        mix(4)
        mix(5)
        turn_back(0)
        mix(6)
        mix(7)
        turn_back(1)
        mix(0)
        mix(1)
        turn_back(2)
        mix(2)
        turn_back(3)
        mix(3)
        turn_back(4)
        second_product(0)
        second_product(1)
        second_product(2)
        second_product(3)
        second_product(4)
